import numpy as np
import ml_dtypes


def mxq(x, axis, fmt="e4m3"):
    dtype, down = {"e4m3": (ml_dtypes.float8_e4m3fn, 7), "e5m2": (ml_dtypes.float8_e5m2, 14)}[fmt]
    v = np.moveaxis(np.asarray(x, np.float32).astype(ml_dtypes.bfloat16).astype(np.float64), axis, -1)
    blocks = v.reshape(v.shape[:-1] + (-1, 32))
    amax = np.abs(blocks).max(-1, keepdims=True)
    byte = np.maximum(np.where(amax > 0, np.frexp(amax)[1] - 1 + 127, 0) - down, 1)
    scale = np.exp2(byte - 127.0)
    codes = (blocks / scale).astype(np.float32).astype(dtype).astype(np.float64)
    return np.moveaxis((codes * scale).reshape(v.shape), -1, axis)


WIDE = False


def mx_kscale(k, group=512):
    if not WIDE:
        return np.ones(k)
    levels = np.array([18, -18])
    if group != 512:
        return np.exp2(np.random.permutation(np.resize(levels, k // group))).repeat(group)
    if k % 512:
        return np.exp2(np.random.permutation(np.resize(levels, k // 32))).repeat(32)
    a = np.empty((k // 512, 16))
    for p in range(k // 512):
        a[p, :8] = np.random.permutation(np.resize(levels, 8))
        for g in range(8):
            far = levels[np.abs(levels - a[p, g]) >= 10]
            a[p, g + 8] = far[np.random.randint(len(far))]
    return np.exp2(a.ravel()).repeat(32)


def f64(x):
    return np.asarray(x).astype(np.float64)


E2M1 = np.array([0.0, 0.5, 1.0, 1.5, 2.0, 3.0, 4.0, 6.0, -0.0, -0.5, -1.0, -1.5, -2.0, -3.0, -4.0, -6.0])


def pack_group(w):
    k, n = w.shape
    w = f64(np.asarray(w, np.float32).astype(ml_dtypes.bfloat16)).reshape(k // 32, 32, n)
    amax = np.abs(w).max(1)
    mant, ex = np.frexp(amax / 6.0)
    byte = np.clip(np.where(amax > 0, np.where(mant > 0.5, ex, ex - 1) + 127, 1), 1, 254)
    scaled = (w * np.exp2(127.0 - byte)[:, None, :]).reshape(k, n).astype(np.float32)
    c = np.ascontiguousarray(scaled.reshape(k // 4, 4, n).transpose(0, 2, 1)).astype(ml_dtypes.float4_e2m1fn).view(np.uint8) & 0xF
    return np.ascontiguousarray((c[..., 0::2] | (c[..., 1::2] << 4)).reshape(k // 4, 2 * n)), byte.astype(np.uint8)


def unpack_group(words, scales):
    p, n = words.shape[0], scales.shape[1]
    words = np.ascontiguousarray(words).reshape(p, n, 2)
    nib = np.empty((p, n, 4), np.uint8)
    nib[..., 0::2] = words & 0xF
    nib[..., 1::2] = words >> 4
    return E2M1[nib].transpose(0, 2, 1).reshape(4 * p, n) * np.repeat(np.exp2(scales.astype(np.float64) - 127.0), 32, axis=0)


G, D, M, N = 4, 128, 256, 1024


def setup_inputs():
    n = np.random.standard_normal
    s = mx_kscale(D, 0)[:, None]
    w_ = [pack_group(w) for w in n((G, D, M)) / np.sqrt(D) / s]
    return {
        "x": (n((G, D, N)) * s).astype(np.float32),
        "w_words": np.stack([w[0] for w in w_]),
        "w_scales": np.stack([w[1] for w in w_]),
        "b": (0.5 * n((G, M, 1))).astype(np.float32),
    }


def reference(x, w_words, w_scales, b):
    xq = mxq(f64(x), 1, "e4m3")
    y = np.stack([unpack_group(w_words[g], w_scales[g]) for g in range(G)]).transpose(0, 2, 1) @ xq
    y = y + f64(b)
    y = 1.0 / (1.0 + np.exp(-(y)))
    return y

@@ -1,0 +1,117 @@
+from contextlib import ExitStack
+
+import concourse.mybir as mybir
+
+G, D, M, N = 4, 128, 256, 1024
+FLOPS = 2 * G * D * M * N
+
+F32 = mybir.dt.float32
+BF16 = mybir.dt.bfloat16
+I32 = mybir.dt.int32
+U32 = mybir.dt.uint32
+U8 = mybir.dt.uint8
+FP8X4 = mybir.dt.float8_e4m3fn_x4
+FP4X4 = mybir.dt.float4_e2m1fn_x4
+SIGMOID = mybir.ActivationFunctionType.Sigmoid
+
+P = 128
+PACK = 4
+ROWS = D // PACK
+BLOCKS = D // 32
+M_TILE = 128
+M_TILES = M // M_TILE
+N_TILE = 512
+PIECE = 256
+LOADS = [(0, 256), (256, 512), (512, 1024)]
+
+
+def tile_rows_glin_sigmoid_bias_kernel(tc, x, w_words, w_scales, b, out):
+    nc = tc.nc
+    with ExitStack() as ctx:
+        keep = ctx.enter_context(tc.tile_pool(name="keep", bufs=1))
+        psum = ctx.enter_context(tc.psum_pool(name="psum", bufs=1))
+        ctx.enter_context(tc.manual_schedule())
+
+        x_rows = x.rearrange("g (p j) n -> (g p) j n", j=PACK)
+        raw = []
+        for i, (lo, hi) in enumerate(LOADS):
+            t = keep.tile([P, PACK, hi - lo], F32, name="raw%d" % i)
+            nc.sync.dma_start(out=t[:], in_=x_rows[:, :, lo:hi])
+            raw.append(t)
+
+        w_sb = keep.tile([P, 2 * M], U8, align_bytes=64)
+        ws_sb = keep.tile([P, M], U8, align_bytes=64)
+        b_rows = keep.tile([P, G * M_TILES * 32], F32, align_bytes=64)
+        b_cols = keep.tile([P, G * M_TILES * 32], F32, align_bytes=64)
+        nc.gpsimd.memset(ws_sb[:].bitcast(I32), 0)
+        nc.vector.memset(b_rows[:], 0.0)
+        nc.scalar.dma_start(out=w_sb[:].bitcast(I32), in_=w_words.rearrange("g p c -> (g p) c").bitcast(I32))
+        for f in range(BLOCKS):
+            nc.scalar.dma_start(out=ws_sb[f:P:ROWS, :].bitcast(I32), in_=w_scales[:, f, :].bitcast(I32))
+        nc.scalar.dma_start(
+            out=b_rows[0:P:32, :].rearrange("q (t c) -> q t c", c=32),
+            in_=b.rearrange("g (h q c) o -> q (g h) (c o)", h=M_TILES, c=32),
+        )
+
+        halves = N // N_TILE
+        codes = [keep.tile([P, N_TILE], U32, align_bytes=64, name="codes%d" % h) for h in range(halves)]
+        scales = [keep.tile([P, N_TILE], U8, align_bytes=64, name="scales%d" % h) for h in range(halves)]
+        grouped = [keep.tile([P, PIECE * PACK], BF16, align_bytes=64, name="grouped%d" % k) for k in range(N // PIECE)]
+        banks = {}
+        for g in range(G):
+            for mt in range(M_TILES):
+                banks[g, mt] = psum.tile([M_TILE, N_TILE], F32, name="bank%d_%d" % (g, mt))
+
+        def interleave(k):
+            n0 = k * PIECE
+            i = max(j for j in range(len(LOADS)) if LOADS[j][0] <= n0)
+            off = n0 - LOADS[i][0]
+            nc.vector.tensor_copy(
+                out=grouped[k][:].rearrange("p (c j) -> p c j", j=PACK),
+                in_=raw[i][:, :, off : off + PIECE].rearrange("p j c -> p c j"),
+            )
+
+        def quantize(k):
+            h, off = divmod(k * PIECE, N_TILE)
+            nc.vector.quantize_mx(
+                out=codes[h][:, off : off + PIECE].bitcast(FP8X4),
+                scales=scales[h][:, off : off + PIECE],
+                in_=grouped[k][:],
+            )
+
+        def multiply(g, mt, h):
+            rows = slice(ROWS * g, ROWS * (g + 1))
+            nc.tensor.matmul_mx(
+                out=banks[g, mt][:],
+                lhsT=w_sb[rows, 2 * M_TILE * mt : 2 * M_TILE * (mt + 1)].bitcast(FP4X4),
+                lhsT_scale=ws_sb[rows, M_TILE * mt : M_TILE * (mt + 1)],
+                rhs=codes[h][rows, :].bitcast(FP8X4),
+                rhs_scale=scales[h][rows, :],
+                start=True,
+                stop=True,
+            )
+
+        def finish(g, mt, h):
+            res = keep.tile([M_TILE, N_TILE], F32, name="res%d_%d_%d" % (g, mt, h))
+            col = 32 * (g * M_TILES + mt)
+            nc.scalar.activation(out=res[:], in_=banks[g, mt][:], func=SIGMOID, bias=b_cols[:, col : col + 1])
+            nc.sync.dma_start(out=out[g, M_TILE * mt : M_TILE * (mt + 1), N_TILE * h : N_TILE * (h + 1)], in_=res[:])
+
+        order = [(g, mt) for mt in range(M_TILES) for g in range(G)]
+
+        interleave(0)
+        quantize(0)
+        interleave(1)
+        quantize(1)
+        nc.vector.transpose(out=b_cols[:], in_=b_rows[:])
+        for g, mt in order:
+            multiply(g, mt, 0)
+        interleave(2)
+        interleave(3)
+        quantize(2)
+        quantize(3)
+        for g, mt in order:
+            finish(g, mt, 0)
+            multiply(g, mt, 1)
+        for g, mt in order:
+            finish(g, mt, 1)

@@ -32,6 +32,16 @@ def tile_rows_glin_sigmoid_bias_kernel(tc, x, w_words, w_scales, b, out):
         psum = ctx.enter_context(tc.psum_pool(name="psum", bufs=1))
         ctx.enter_context(tc.manual_schedule())
 
+        w_sb = keep.tile([P, 2 * M], U8, align_bytes=64)
+        ws_sb = keep.tile([P, M], U8, align_bytes=64)
+        b_rows = keep.tile([P, G * M_TILES * 32], F32, align_bytes=64)
+        b_cols = keep.tile([P, G * M_TILES * 32], F32, align_bytes=64)
+        codes = keep.tile([P, PIECE + N], U32, align_bytes=64)
+        scales = keep.tile([P, PIECE + N], U8, align_bytes=64)
+        warm_in = keep.tile([P, 1], F32)
+        warm_out = keep.tile([P, 1], F32)
+
+        nc.scalar.dma_start(out=w_sb[:].bitcast(I32), in_=w_words.rearrange("g p c -> (g p) c").bitcast(I32))
         x_rows = x.rearrange("g (p j) n -> (g p) j n", j=PACK)
         raw = []
         for i, (lo, hi) in enumerate(LOADS):
@@ -39,28 +49,24 @@ def tile_rows_glin_sigmoid_bias_kernel(tc, x, w_words, w_scales, b, out):
             nc.sync.dma_start(out=t[:], in_=x_rows[:, :, lo:hi])
             raw.append(t)
 
-        w_sb = keep.tile([P, 2 * M], U8, align_bytes=64)
-        ws_sb = keep.tile([P, M], U8, align_bytes=64)
-        b_rows = keep.tile([P, G * M_TILES * 32], F32, align_bytes=64)
-        b_cols = keep.tile([P, G * M_TILES * 32], F32, align_bytes=64)
-        nc.gpsimd.memset(ws_sb[:].bitcast(I32), 0)
-        nc.vector.memset(b_rows[:], 0.0)
-        nc.scalar.dma_start(out=w_sb[:].bitcast(I32), in_=w_words.rearrange("g p c -> (g p) c").bitcast(I32))
-        for f in range(BLOCKS):
-            nc.scalar.dma_start(out=ws_sb[f:P:ROWS, :].bitcast(I32), in_=w_scales[:, f, :].bitcast(I32))
-        nc.scalar.dma_start(
+        nc.vector.memset(ws_sb[:].bitcast(I32), 0)
+        nc.vector.memset(warm_in[:], 0.0)
+        nc.gpsimd.memset(b_rows[:], 0.0)
+        nc.gpsimd.dma_start(
             out=b_rows[0:P:32, :].rearrange("q (t c) -> q t c", c=32),
             in_=b.rearrange("g (h q c) o -> q (g h) (c o)", h=M_TILES, c=32),
         )
+        for f in range(BLOCKS):
+            nc.scalar.dma_start(out=ws_sb[f:P:ROWS, :].bitcast(I32), in_=w_scales[:, f, :].bitcast(I32))
+        nc.scalar.activation(out=warm_out[:], in_=warm_in[:], func=SIGMOID)
+        nc.vector.memset(codes[:, 0:PIECE], 0)
+        nc.vector.memset(scales[:, 0:PIECE].bitcast(U32), 0)
 
-        halves = N // N_TILE
-        codes = [keep.tile([P, N_TILE], U32, align_bytes=64, name="codes%d" % h) for h in range(halves)]
-        scales = [keep.tile([P, N_TILE], U8, align_bytes=64, name="scales%d" % h) for h in range(halves)]
         grouped = [keep.tile([P, PIECE * PACK], BF16, align_bytes=64, name="grouped%d" % k) for k in range(N // PIECE)]
         banks = {}
         for g in range(G):
-            for mt in range(M_TILES):
-                banks[g, mt] = psum.tile([M_TILE, N_TILE], F32, name="bank%d_%d" % (g, mt))
+            for i in range(2):
+                banks[g, i] = psum.tile([M_TILE, N_TILE], F32, name="bank%d_%d" % (g, i))
 
         def interleave(k):
             n0 = k * PIECE
@@ -72,46 +78,44 @@ def tile_rows_glin_sigmoid_bias_kernel(tc, x, w_words, w_scales, b, out):
             )
 
         def quantize(k):
-            h, off = divmod(k * PIECE, N_TILE)
-            nc.vector.quantize_mx(
-                out=codes[h][:, off : off + PIECE].bitcast(FP8X4),
-                scales=scales[h][:, off : off + PIECE],
-                in_=grouped[k][:],
-            )
+            cols = slice(PIECE * (k + 1), PIECE * (k + 2))
+            nc.vector.quantize_mx(out=codes[:, cols].bitcast(FP8X4), scales=scales[:, cols], in_=grouped[k][:])
 
-        def multiply(g, mt, h):
+        def multiply(g, mt, end, bank):
             rows = slice(ROWS * g, ROWS * (g + 1))
+            cols = slice(PIECE + end - N_TILE, PIECE + end)
             nc.tensor.matmul_mx(
-                out=banks[g, mt][:],
+                out=banks[g, bank][:],
                 lhsT=w_sb[rows, 2 * M_TILE * mt : 2 * M_TILE * (mt + 1)].bitcast(FP4X4),
                 lhsT_scale=ws_sb[rows, M_TILE * mt : M_TILE * (mt + 1)],
-                rhs=codes[h][rows, :].bitcast(FP8X4),
-                rhs_scale=scales[h][rows, :],
+                rhs=codes[rows, cols].bitcast(FP8X4),
+                rhs_scale=scales[rows, cols],
                 start=True,
                 stop=True,
             )
 
-        def finish(g, mt, h):
-            res = keep.tile([M_TILE, N_TILE], F32, name="res%d_%d_%d" % (g, mt, h))
+        def finish(g, mt, begin, end, bank):
+            width = end - begin
+            res = keep.tile([M_TILE, width], F32, name="res%d_%d_%d" % (g, mt, begin))
             col = 32 * (g * M_TILES + mt)
-            nc.scalar.activation(out=res[:], in_=banks[g, mt][:], func=SIGMOID, bias=b_cols[:, col : col + 1])
-            nc.sync.dma_start(out=out[g, M_TILE * mt : M_TILE * (mt + 1), N_TILE * h : N_TILE * (h + 1)], in_=res[:])
+            nc.scalar.activation(
+                out=res[:], in_=banks[g, bank][:, N_TILE - width :], func=SIGMOID, bias=b_cols[:, col : col + 1]
+            )
+            nc.sync.dma_start(out=out[g, M_TILE * mt : M_TILE * (mt + 1), begin:end], in_=res[:])
 
-        order = [(g, mt) for mt in range(M_TILES) for g in range(G)]
+        rounds = [(0, 0, 256), (1, 0, 512), (0, 256, 512), (0, 512, 1024), (1, 512, 1024)]
 
         interleave(0)
         quantize(0)
+        nc.vector.transpose(out=b_cols[:], in_=b_rows[:])
         interleave(1)
         quantize(1)
-        nc.vector.transpose(out=b_cols[:], in_=b_rows[:])
-        for g, mt in order:
-            multiply(g, mt, 0)
         interleave(2)
         interleave(3)
         quantize(2)
         quantize(3)
-        for g, mt in order:
-            finish(g, mt, 0)
-            multiply(g, mt, 1)
-        for g, mt in order:
-            finish(g, mt, 1)
+        for r, (mt, begin, end) in enumerate(rounds):
+            for g in range(G):
+                multiply(g, mt, end, r % 2)
+            for g in range(G):
+                finish(g, mt, begin, end, r % 2)

@@ -22,6 +22,7 @@ M_TILE = 128
 M_TILES = M // M_TILE
 N_TILE = 512
 PIECE = 256
+SPLIT = 168
 LOADS = [(0, 256), (256, 512), (512, 1024)]
 
 
@@ -41,24 +42,27 @@ def tile_rows_glin_sigmoid_bias_kernel(tc, x, w_words, w_scales, b, out):
         warm_in = keep.tile([P, 1], F32)
         warm_out = keep.tile([P, 1], F32)
 
-        nc.scalar.dma_start(out=w_sb[:].bitcast(I32), in_=w_words.rearrange("g p c -> (g p) c").bitcast(I32))
         x_rows = x.rearrange("g (p j) n -> (g p) j n", j=PACK)
-        raw = []
-        for i, (lo, hi) in enumerate(LOADS):
-            t = keep.tile([P, PACK, hi - lo], F32, name="raw%d" % i)
-            nc.sync.dma_start(out=t[:], in_=x_rows[:, :, lo:hi])
-            raw.append(t)
+        raw = [keep.tile([P, PACK, hi - lo], F32, name="raw%d" % i) for i, (lo, hi) in enumerate(LOADS)]
+
+        def load(i):
+            lo, hi = LOADS[i]
+            nc.sync.dma_start(out=raw[i][:], in_=x_rows[:, :, lo:hi])
 
         nc.vector.memset(ws_sb[:].bitcast(I32), 0)
-        nc.vector.memset(warm_in[:], 0.0)
         nc.gpsimd.memset(b_rows[:], 0.0)
-        nc.gpsimd.dma_start(
+        nc.vector.memset(warm_in[:], 0.0)
+        nc.scalar.activation(out=warm_out[:], in_=warm_in[:], func=SIGMOID)
+        load(0)
+        nc.sync.dma_start(out=w_sb[:].bitcast(I32), in_=w_words.rearrange("g p c -> (g p) c").bitcast(I32))
+        for f in range(BLOCKS):
+            nc.sync.dma_start(out=ws_sb[f:P:ROWS, :].bitcast(I32), in_=w_scales[:, f, :].bitcast(I32))
+        nc.sync.dma_start(
             out=b_rows[0:P:32, :].rearrange("q (t c) -> q t c", c=32),
             in_=b.rearrange("g (h q c) o -> q (g h) (c o)", h=M_TILES, c=32),
         )
-        for f in range(BLOCKS):
-            nc.scalar.dma_start(out=ws_sb[f:P:ROWS, :].bitcast(I32), in_=w_scales[:, f, :].bitcast(I32))
-        nc.scalar.activation(out=warm_out[:], in_=warm_in[:], func=SIGMOID)
+        load(1)
+        load(2)
         nc.vector.memset(codes[:, 0:PIECE], 0)
         nc.vector.memset(scales[:, 0:PIECE].bitcast(U32), 0)
 
@@ -68,13 +72,13 @@ def tile_rows_glin_sigmoid_bias_kernel(tc, x, w_words, w_scales, b, out):
             for i in range(2):
                 banks[g, i] = psum.tile([M_TILE, N_TILE], F32, name="bank%d_%d" % (g, i))
 
-        def interleave(k):
+        def interleave(copy, k, lo, hi):
             n0 = k * PIECE
             i = max(j for j in range(len(LOADS)) if LOADS[j][0] <= n0)
             off = n0 - LOADS[i][0]
-            nc.vector.tensor_copy(
-                out=grouped[k][:].rearrange("p (c j) -> p c j", j=PACK),
-                in_=raw[i][:, :, off : off + PIECE].rearrange("p j c -> p c j"),
+            copy(
+                out=grouped[k][:, PACK * lo : PACK * hi].rearrange("p (c i j) -> p c j i", i=4, j=PACK),
+                in_=raw[i][:, :, off + lo : off + hi].rearrange("p j (c i) -> p c j i", i=4),
             )
 
         def quantize(k):
@@ -105,13 +109,14 @@ def tile_rows_glin_sigmoid_bias_kernel(tc, x, w_words, w_scales, b, out):
 
         rounds = [(0, 0, 256), (1, 0, 512), (0, 256, 512), (0, 512, 1024), (1, 512, 1024)]
 
-        interleave(0)
+        interleave(nc.vector.tensor_copy, 0, 0, SPLIT)
+        interleave(nc.scalar.copy, 0, SPLIT, PIECE)
         quantize(0)
         nc.vector.transpose(out=b_cols[:], in_=b_rows[:])
-        interleave(1)
+        interleave(nc.vector.tensor_copy, 1, 0, PIECE)
         quantize(1)
-        interleave(2)
-        interleave(3)
+        interleave(nc.vector.tensor_copy, 2, 0, PIECE)
+        interleave(nc.vector.tensor_copy, 3, 0, PIECE)
         quantize(2)
         quantize(3)
         for r, (mt, begin, end) in enumerate(rounds):

from contextlib import ExitStack

import concourse.mybir as mybir

G, D, M, N = 4, 128, 256, 1024
FLOPS = 2 * G * D * M * N

F32 = mybir.dt.float32
BF16 = mybir.dt.bfloat16
I32 = mybir.dt.int32
U32 = mybir.dt.uint32
U8 = mybir.dt.uint8
FP8X4 = mybir.dt.float8_e4m3fn_x4
FP4X4 = mybir.dt.float4_e2m1fn_x4
SIGMOID = mybir.ActivationFunctionType.Sigmoid

P = 128
PACK = 4
ROWS = D // PACK
BLOCKS = D // 32
M_TILE = 128
M_TILES = M // M_TILE
N_TILE = 512
PIECE = 256
SPLIT = 168
LOADS = [(0, 256), (256, 512), (512, 1024)]


def tile_rows_glin_sigmoid_bias_kernel(tc, x, w_words, w_scales, b, out):
    nc = tc.nc
    with ExitStack() as ctx:
        keep = ctx.enter_context(tc.tile_pool(name="keep", bufs=1))
        psum = ctx.enter_context(tc.psum_pool(name="psum", bufs=1))
        ctx.enter_context(tc.manual_schedule())

        w_sb = keep.tile([P, 2 * M], U8, align_bytes=64)
        ws_sb = keep.tile([P, M], U8, align_bytes=64)
        b_rows = keep.tile([P, G * M_TILES * 32], F32, align_bytes=64)
        b_cols = keep.tile([P, G * M_TILES * 32], F32, align_bytes=64)
        codes = keep.tile([P, PIECE + N], U32, align_bytes=64)
        scales = keep.tile([P, PIECE + N], U8, align_bytes=64)
        warm_in = keep.tile([P, 1], F32)
        warm_out = keep.tile([P, 1], F32)

        x_rows = x.rearrange("g (p j) n -> (g p) j n", j=PACK)
        raw = [keep.tile([P, PACK, hi - lo], F32, name="raw%d" % i) for i, (lo, hi) in enumerate(LOADS)]

        def load(i):
            lo, hi = LOADS[i]
            nc.sync.dma_start(out=raw[i][:], in_=x_rows[:, :, lo:hi])

        nc.vector.memset(ws_sb[:].bitcast(I32), 0)
        nc.gpsimd.memset(b_rows[:], 0.0)
        nc.vector.memset(warm_in[:], 0.0)
        nc.scalar.activation(out=warm_out[:], in_=warm_in[:], func=SIGMOID)
        load(0)
        nc.sync.dma_start(out=w_sb[:].bitcast(I32), in_=w_words.rearrange("g p c -> (g p) c").bitcast(I32))
        for f in range(BLOCKS):
            nc.sync.dma_start(out=ws_sb[f:P:ROWS, :].bitcast(I32), in_=w_scales[:, f, :].bitcast(I32))
        nc.sync.dma_start(
            out=b_rows[0:P:32, :].rearrange("q (t c) -> q t c", c=32),
            in_=b.rearrange("g (h q c) o -> q (g h) (c o)", h=M_TILES, c=32),
        )
        load(1)
        load(2)
        nc.vector.memset(codes[:, 0:PIECE], 0)
        nc.vector.memset(scales[:, 0:PIECE].bitcast(U32), 0)

        grouped = [keep.tile([P, PIECE * PACK], BF16, align_bytes=64, name="grouped%d" % k) for k in range(N // PIECE)]
        banks = {}
        for g in range(G):
            for i in range(2):
                banks[g, i] = psum.tile([M_TILE, N_TILE], F32, name="bank%d_%d" % (g, i))

        def interleave(copy, k, lo, hi):
            n0 = k * PIECE
            i = max(j for j in range(len(LOADS)) if LOADS[j][0] <= n0)
            off = n0 - LOADS[i][0]
            copy(
                out=grouped[k][:, PACK * lo : PACK * hi].rearrange("p (c i j) -> p c j i", i=4, j=PACK),
                in_=raw[i][:, :, off + lo : off + hi].rearrange("p j (c i) -> p c j i", i=4),
            )

        def quantize(k):
            cols = slice(PIECE * (k + 1), PIECE * (k + 2))
            nc.vector.quantize_mx(out=codes[:, cols].bitcast(FP8X4), scales=scales[:, cols], in_=grouped[k][:])

        def multiply(g, mt, end, bank):
            rows = slice(ROWS * g, ROWS * (g + 1))
            cols = slice(PIECE + end - N_TILE, PIECE + end)
            nc.tensor.matmul_mx(
                out=banks[g, bank][:],
                lhsT=w_sb[rows, 2 * M_TILE * mt : 2 * M_TILE * (mt + 1)].bitcast(FP4X4),
                lhsT_scale=ws_sb[rows, M_TILE * mt : M_TILE * (mt + 1)],
                rhs=codes[rows, cols].bitcast(FP8X4),
                rhs_scale=scales[rows, cols],
                start=True,
                stop=True,
            )

        def finish(g, mt, begin, end, bank):
            width = end - begin
            res = keep.tile([M_TILE, width], F32, name="res%d_%d_%d" % (g, mt, begin))
            col = 32 * (g * M_TILES + mt)
            nc.scalar.activation(
                out=res[:], in_=banks[g, bank][:, N_TILE - width :], func=SIGMOID, bias=b_cols[:, col : col + 1]
            )
            nc.sync.dma_start(out=out[g, M_TILE * mt : M_TILE * (mt + 1), begin:end], in_=res[:])

        rounds = [(0, 0, 256), (1, 0, 512), (0, 256, 512), (0, 512, 1024), (1, 512, 1024)]

        interleave(nc.vector.tensor_copy, 0, 0, SPLIT)
        interleave(nc.scalar.copy, 0, SPLIT, PIECE)
        quantize(0)
        nc.vector.transpose(out=b_cols[:], in_=b_rows[:])
        interleave(nc.vector.tensor_copy, 1, 0, PIECE)
        quantize(1)
        interleave(nc.vector.tensor_copy, 2, 0, PIECE)
        interleave(nc.vector.tensor_copy, 3, 0, PIECE)
        quantize(2)
        quantize(3)
        for r, (mt, begin, end) in enumerate(rounds):
            for g in range(G):
                multiply(g, mt, end, r % 2)
            for g in range(G):
                finish(g, mt, begin, end, r % 2)
